import numpy as np
import ml_dtypes


def mxq(x, axis, fmt="e4m3"):
    dtype, down = {"e4m3": (ml_dtypes.float8_e4m3fn, 7), "e5m2": (ml_dtypes.float8_e5m2, 14)}[fmt]
    v = np.moveaxis(np.asarray(x, np.float32).astype(ml_dtypes.bfloat16).astype(np.float64), axis, -1)
    blocks = v.reshape(v.shape[:-1] + (-1, 32))
    amax = np.abs(blocks).max(-1, keepdims=True)
    byte = np.maximum(np.where(amax > 0, np.frexp(amax)[1] - 1 + 127, 0) - down, 1)
    scale = np.exp2(byte - 127.0)
    codes = (blocks / scale).astype(np.float32).astype(dtype).astype(np.float64)
    return np.moveaxis((codes * scale).reshape(v.shape), -1, axis)


WIDE = False


def mx_kscale(k):
    if not WIDE:
        return np.ones(k)
    levels = np.array([10, -10, 5, -5, 0])
    if k % 512:
        return np.exp2(np.random.permutation(np.resize(levels, k // 32))).repeat(32)
    a = np.empty((k // 512, 16))
    for p in range(k // 512):
        a[p, :8] = np.random.permutation(np.resize(levels, 8))
        for g in range(8):
            far = levels[np.abs(levels - a[p, g]) >= 10]
            a[p, g + 8] = far[np.random.randint(len(far))]
    return np.exp2(a.ravel()).repeat(32)


def f64(x):
    return np.asarray(x).astype(np.float64)


def striped(idx):
    return np.tile(idx.reshape(-1, 16).T, (8, 1)).astype(np.uint16)


def unstriped(offs):
    return offs[:16].T.reshape(-1).astype(np.int64)


E2M1 = np.array([0.0, 0.5, 1.0, 1.5, 2.0, 3.0, 4.0, 6.0, -0.0, -0.5, -1.0, -1.5, -2.0, -3.0, -4.0, -6.0])


def pack_weight(w, fmt):
    k, n = w.shape
    w = f64(np.asarray(w, np.float32).astype(ml_dtypes.bfloat16)).reshape(k // 32, 32, n)
    amax = np.abs(w).max(1)
    if fmt == "e4m3":
        byte = np.frexp(amax)[1] - 1 + 127 - 7
    else:
        mant, ex = np.frexp(amax / 6.0)
        byte = np.where(mant > 0.5, ex, ex - 1) + 127
    byte = np.clip(np.where(amax > 0, byte, 1), 1, 254)
    scaled = (w * np.exp2(127.0 - byte)[:, None, :]).reshape(k, n).astype(np.float32)
    by_word = np.ascontiguousarray(scaled.reshape(k // 512, 128, 4, n).transpose(0, 1, 3, 2))
    if fmt == "e4m3":
        words = by_word.astype(ml_dtypes.float8_e4m3fn).view(np.uint8)
    else:
        c = by_word.astype(ml_dtypes.float4_e2m1fn).view(np.uint8) & 0xF
        words = (c[..., 0::2] | (c[..., 1::2] << 4)).reshape(k // 512, 128, 2 * n)
    return np.ascontiguousarray(words), np.ascontiguousarray(byte.astype(np.uint8).reshape(k // 512, 16, n))


def unpack_weight(words, scales, fmt):
    g, _, n = scales.shape
    words = np.ascontiguousarray(words).reshape(g, 128, n, -1)
    if fmt == "e4m3":
        vals = words.view(ml_dtypes.float8_e4m3fn).astype(np.float64)
    else:
        nib = np.empty((g, 128, n, 4), np.uint8)
        nib[..., 0::2] = words & 0xF
        nib[..., 1::2] = words >> 4
        vals = E2M1[nib]
    vals = vals * np.repeat(np.exp2(scales.astype(np.float64) - 127.0), 8, axis=1)[..., None]
    return vals.transpose(0, 1, 3, 2).reshape(g * 512, n)


def gelu(v):
    return 0.5 * v * (1.0 + np.tanh(np.sqrt(2.0 / np.pi) * (v + 0.044715 * v**3)))


K, T, S, P, P2, H, N = 1536, 4096, 1024, 512, 256, 512, 512


def setup_inputs():
    n = np.random.standard_normal
    s = mx_kscale(K)[:, None]
    u = mx_kscale(H)[:, None]
    tab_words, tab_scales = pack_weight(n((K, T)) * s, "e4m3")
    w1_words, w1_scales = pack_weight(n((K, H)) / np.sqrt(K) / s * u.T, "e2m1")
    w2 = 0.54 * n((K, H)) / np.sqrt(K) / s
    w3 = 0.7 * n((H, N)) / np.sqrt(H) / u
    return {
        "tab_words": tab_words, "tab_scales": tab_scales,
        "offs": striped(np.random.permutation(T)[:S]),
        "pos1": striped(np.random.permutation(S)[:P]),
        "pos2": striped(np.random.permutation(S)[:P]),
        "pos3": striped(np.random.permutation(P)[:P2]),
        "pos4": striped(np.random.permutation(S)[:P2]),
        "w1_words": w1_words, "w1_scales": w1_scales,
        "w2": w2.astype(np.float32),
        "w3": w3.astype(np.float32),
        "gain": np.exp(0.3 * n(N)).astype(np.float32),
    }


def reference(tab_words, tab_scales, offs, pos1, pos2, pos3, pos4, w1_words, w1_scales, w2, w3, gain):
    v = unpack_weight(tab_words, tab_scales, "e4m3")[:, unstriped(offs)]
    w1 = unpack_weight(w1_words, w1_scales, "e2m1")
    f = w1.T @ v
    b = mxq(f64(w2), 0, "e4m3").T @ v
    h = f + f * np.sin(b)
    a1 = np.maximum(h[:, unstriped(pos1)], h[:, unstriped(pos2)])
    a2 = a1[:, unstriped(pos3)] - h[:, unstriped(pos4)]
    y = mxq(f64(w3), 0, "e4m3").T @ mxq(a2, 0, "e4m3")
    return f64(gain)[:, None] * np.tanh(y)

@@ -1,0 +1,274 @@
+import math
+from contextlib import ExitStack
+
+import concourse.mybir as mybir
+
+K, T, S, P1, P2, H, N = 1536, 4096, 1024, 512, 256, 512, 512
+FLOPS = 2 * K * H * S * 2 + 2 * H * N * P2
+
+F32 = mybir.dt.float32
+BF16 = mybir.dt.bfloat16
+I32 = mybir.dt.int32
+U32 = mybir.dt.uint32
+U16 = mybir.dt.uint16
+U8 = mybir.dt.uint8
+FP8X4 = mybir.dt.float8_e4m3fn_x4
+FP4X4 = mybir.dt.float4_e2m1fn_x4
+ACT = mybir.ActivationFunctionType
+ALU = mybir.AluOpType
+
+P = 128
+PACK = 4
+PASSES = K // (P * PACK)
+HALF = 512
+BLOCKS = 16
+RUN = 8
+
+
+def tile_list_shell_company_leads_kernel(
+    tc, tab_words, tab_scales, offs, pos1, pos2, pos3, pos4, w1_words, w1_scales, w2, w3, gain, out
+):
+    nc = tc.nc
+    with ExitStack() as ctx:
+        keep = ctx.enter_context(tc.tile_pool(name="keep", bufs=1))
+        ring = ctx.enter_context(tc.tile_pool(name="ring", bufs=2))
+        psum = ctx.enter_context(tc.psum_pool(name="psum", bufs=2))
+
+        def held(shape, dtype, name):
+            return keep.tile(shape, dtype, name=name, align_bytes=64)
+
+        offs_t = held([P, S // 16], U16, "offs_t")
+        pos1_t = held([P, P1 // 16], U16, "pos1_t")
+        pos2_t = held([P, P1 // 16], U16, "pos2_t")
+        pos3_t = held([P, P2 // 16], U16, "pos3_t")
+        pos4_t = held([P, P2 // 16], U16, "pos4_t")
+
+        scale_rows = held([P, T], U8, "scale_rows")
+        picked_rows = held([P, S], U8, "picked_rows")
+        v_scales = held([P, PASSES * S], U8, "v_scales")
+        w1_scales_raw = held([P, PASSES * H], U8, "w1_scales_raw")
+        w1_scales_t = held([P, PASSES * H], U8, "w1_scales_t")
+        w1_raw = held([P, PASSES * 2 * H], U8, "w1_raw")
+        w1_codes = held([P, PASSES * 2 * H], U8, "w1_codes")
+        table = [held([P, T], U32, f"table{a}") for a in range(PASSES)]
+        first_row = P - 16 * PASSES
+        v_codes = [[held([P, HALF], U32, f"v_codes{a}_{u}") for u in range(2)] for a in range(PASSES)]
+        w2_raw = [held([P, PACK, H], F32, f"w2_raw{a}") for a in range(PASSES)]
+        gain_t = held([P, PACK], F32, "gain_t")
+        ones = held([P, 1], F32, "ones")
+        shift = held([P, 1], F32, "shift")
+
+        nc.vector.memset(scale_rows[0:first_row, :].bitcast(I32), 0)
+        nc.gpsimd.memset(w1_scales_raw[:].bitcast(I32), 0)
+        nc.gpsimd.memset(v_scales[:].bitcast(I32), 0)
+        nc.gpsimd.memset(ones[:], 1.0)
+        nc.gpsimd.tensor_scalar(shift[:], ones[:], -math.pi / 8, 0.0, ALU.mult, ALU.add)
+
+        def load_table(a):
+            nc.sync.dma_start(
+                out=table[a][:].bitcast(I32), in_=tab_words[a].rearrange("p t i -> p (t i)").bitcast(I32)
+            )
+
+        def load_w2(a):
+            rows = w2[a * P * PACK : (a + 1) * P * PACK, :]
+            nc.sync.dma_start(out=w2_raw[a][:], in_=rows.rearrange("(p j) c -> p j c", j=PACK))
+
+        nc.sync.dma_start(offs_t[:], offs)
+        nc.sync.dma_start(
+            out=scale_rows[first_row:P, :].bitcast(I32),
+            in_=tab_scales.bitcast(I32).rearrange("a q t -> q a t"),
+        )
+        nc.sync.dma_start(pos1_t[:], pos1)
+        nc.sync.dma_start(pos2_t[:], pos2)
+        nc.sync.dma_start(pos4_t[:], pos4)
+        nc.sync.dma_start(pos3_t[:], pos3)
+        for Q in range(4):
+            nc.gpsimd.dma_start(
+                out=w1_scales_raw[32 * Q : 32 * Q + 4, :].bitcast(I32).rearrange("r (a c) -> r a c", a=PASSES),
+                in_=w1_scales.bitcast(I32)[:, 4 * Q : 4 * Q + 4, :].rearrange("a r c -> r a c"),
+            )
+        with nc.allow_non_contiguous_dma(reason="one gain value a partition"):
+            nc.gpsimd.dma_start(out=gain_t[:], in_=gain.rearrange("(c p) -> p c", p=P))
+        nc.sync.dma_start(
+            out=w1_raw[:].bitcast(I32).rearrange("p (a c) -> p a c", a=PASSES),
+            in_=w1_words.bitcast(I32).rearrange("a p c -> p a c"),
+        )
+        load_table(0)
+        load_table(1)
+        load_w2(0)
+        load_table(2)
+        load_w2(1)
+        load_w2(2)
+
+        nc.vector.tensor_copy(picked_rows[:], scale_rows[:].indirect(offs_t[:]))
+        for Q in range(4):
+            nc.scalar.dma_start(
+                out=v_scales[32 * Q : 32 * Q + 4, :].bitcast(I32).rearrange("r (a c) -> r a c", a=PASSES),
+                in_=picked_rows[first_row + 12 * Q : first_row + 12 * Q + 12, :].bitcast(I32),
+            )
+
+        nc.vector.tensor_copy(
+            out=w1_scales_t[:].bitcast(I32).rearrange("p (a t g w) -> p a t g w", a=PASSES, t=PACK, g=BLOCKS),
+            in_=w1_scales_raw[:].bitcast(I32).rearrange("p (a g t w) -> p a t g w", a=PASSES, t=PACK, g=BLOCKS),
+        )
+        nc.vector.tensor_copy(
+            out=w1_codes[:].bitcast(I32).rearrange("p (a t g w) -> p a t g w", a=PASSES, t=PACK, g=BLOCKS),
+            in_=w1_raw[:].bitcast(I32).rearrange("p (a g t w) -> p a t g w", a=PASSES, t=PACK, g=BLOCKS),
+        )
+
+        def gather_words(a):
+            for u in range(2):
+                cols = slice(u * HALF // 16, (u + 1) * HALF // 16)
+                nc.vector.tensor_copy(v_codes[a][u][:], table[a][:].indirect(offs_t[:, cols]))
+
+        w2_bf = [[held([P, P * PACK], BF16, f"w2_bf{a}_{t}") for t in range(PACK)] for a in range(PASSES)]
+        w2_codes = [[held([P, P], U32, f"w2_codes{a}_{t}") for t in range(PACK)] for a in range(PASSES)]
+        w2_scales = [[held([P, P], U8, f"w2_scales{a}_{t}") for t in range(PACK)] for a in range(PASSES)]
+
+        def round_w2(a, t):
+            src = w2_raw[a][:].rearrange("p j (g t h l) -> p t g h j l", t=PACK, h=2, l=4)[:, t]
+            dst = w2_bf[a][t][:].rearrange("p (g h l j) -> p g h j l", h=2, l=4, j=PACK)
+            nc.vector.tensor_copy(out=dst, in_=src)
+
+        def quantise_w2(a, t):
+            nc.vector.quantize_mx(out=w2_codes[a][t][:].bitcast(FP8X4), scales=w2_scales[a][t][:], in_=w2_bf[a][t][:])
+
+        def prepare_w2(a):
+            for t in range(PACK + 1):
+                if t < PACK:
+                    round_w2(a, t)
+                if t > 0:
+                    quantise_w2(a, t - 1)
+
+        banks = {}
+
+        def open_banks(t):
+            for u in range(2):
+                banks["f", t, u] = psum.tile([P, HALF], F32, name=f"f{t}_{u}", tag=f"f{u}")
+                banks["b", t, u] = psum.tile([P, HALF], F32, name=f"b{t}_{u}", tag=f"b{u}")
+
+        def product(kind, t, u, a):
+            if kind == "f":
+                c0 = a * H + t * P
+                lhsT = w1_codes[:, 2 * c0 : 2 * (c0 + P)].bitcast(FP4X4)
+                lhsT_scale = w1_scales_t[:, c0 : c0 + P]
+            else:
+                lhsT = w2_codes[a][t][:].bitcast(FP8X4)
+                lhsT_scale = w2_scales[a][t][:]
+            s0 = a * S + u * HALF
+            nc.tensor.matmul_mx(
+                out=banks[kind, t, u][:],
+                lhsT=lhsT,
+                lhsT_scale=lhsT_scale,
+                rhs=v_codes[a][u][:].bitcast(FP8X4),
+                rhs_scale=v_scales[:, s0 : s0 + HALF],
+                start=(a == 0),
+                stop=(a == PASSES - 1),
+            )
+
+        def products(kind, tiles, a):
+            for t in tiles:
+                for u in range(2):
+                    product(kind, t, u, a)
+
+        h = [held([P, S], F32, f"h{t}") for t in range(PACK)]
+        a1 = [held([P, P1], F32, f"a1_{t}") for t in range(PACK)]
+        a2 = held([P, PACK, P2], F32, "a2")
+
+        def gate(t):
+            s = [ring.tile([P, HALF], F32, name=f"s{u}") for u in range(2)]
+            q = [ring.tile([P, HALF], F32, name=f"q{u}") for u in range(2)]
+            c2 = [ring.tile([P, HALF], F32, name=f"c2_{u}") for u in range(2)]
+            for u in range(2):
+                nc.scalar.activation(s[u][:], banks["b", t, u][:], ACT.Sin, bias=shift[:], scale=0.25)
+            for u in range(2):
+                nc.scalar.activation(q[u][:], s[u][:], ACT.Square)
+            for u in range(2):
+                nc.scalar.activation(c2[u][:], q[u][:], ACT.Square, bias=ones[:], scale=-2.0)
+            for u in range(2):
+                nc.vector.scalar_tensor_tensor(
+                    h[t][:, u * HALF : (u + 1) * HALF], c2[u][:], 2.0, banks["f", t, u][:], ALU.mult, ALU.mult
+                )
+
+        def pairs(t):
+            g1 = ring.tile([P, P1], F32, name="g1")
+            g2 = ring.tile([P, P1], F32, name="g2")
+            g4 = ring.tile([P, P2], F32, name="g4")
+            nc.vector.tensor_copy(g1[:], h[t][:].indirect(pos1_t[:]))
+            nc.vector.tensor_copy(g2[:], h[t][:].indirect(pos2_t[:]))
+            nc.vector.tensor_copy(g4[:], h[t][:].indirect(pos4_t[:]))
+            nc.vector.tensor_tensor(a1[t][:], g1[:], g2[:], ALU.max)
+            return g4
+
+        def differences(t, g4):
+            nc.vector.tensor_tensor(a2[:, t, :], a1[t][:].indirect(pos3_t[:]), g4[:], ALU.subtract)
+
+        open_banks(0)
+        open_banks(1)
+        gather_words(0)
+        products("f", (0, 1), 0)
+        w3_raw = held([P, PACK, N], F32, "table0")
+        for t in range(PACK):
+            nc.sync.dma_start(
+                out=w3_raw[:, t, :], in_=w3.rearrange("(g t i) n -> t g i n", t=PACK, i=RUN)[t]
+            )
+        gather_words(1)
+        products("f", (0, 1), 1)
+        prepare_w2(0)
+        products("b", (0, 1), 0)
+        gather_words(2)
+        products("f", (0, 1), 2)
+        prepare_w2(1)
+        products("b", (0, 1), 1)
+        prepare_w2(2)
+        products("b", (0, 1), 2)
+
+        w3_bf = held([P, N * PACK], BF16, "w3_bf")
+        w3_codes = held([P, N], U32, "w3_codes")
+        w3_scales = held([P, N], U8, "w3_scales")
+
+        memo = {}
+        for t in range(PACK):
+            gate(t)
+            if t + 2 < PACK:
+                open_banks(t + 2)
+                for kind in ("b", "f"):
+                    for a in range(PASSES):
+                        products(kind, (t + 2,), a)
+            if t > 0:
+                differences(t - 1, memo[t - 1])
+            if t == PACK - 1:
+                nc.scalar.copy(
+                    out=w3_bf[:].rearrange("p (c l j) -> p c j l", l=4, j=PACK),
+                    in_=w3_raw[:].rearrange("p j (c l) -> p c j l", l=4),
+                )
+            memo[t] = pairs(t)
+        nc.vector.quantize_mx(out=w3_codes[:].bitcast(FP8X4), scales=w3_scales[:], in_=w3_bf[:])
+        differences(PACK - 1, memo[PACK - 1])
+
+        a2_bf = held([P, P2 * PACK], BF16, "a2_bf")
+        a2_codes = held([P, P2], U32, "a2_codes")
+        a2_scales = held([P, P2], U8, "a2_scales")
+        nc.vector.tensor_copy(
+            out=a2_bf[:].rearrange("p (c l j) -> p c j l", l=4, j=PACK),
+            in_=a2[:].rearrange("p j (c l) -> p c j l", l=4),
+        )
+        nc.vector.quantize_mx(out=a2_codes[:].bitcast(FP8X4), scales=a2_scales[:], in_=a2_bf[:])
+
+        for c, tag in enumerate(("b0", "b1", "f0", "f1")):
+            y = psum.tile([P, P2], F32, name=f"y{c}", tag=tag)
+            nc.tensor.matmul_mx(
+                out=y[:],
+                lhsT=w3_codes[:, c * P : (c + 1) * P].bitcast(FP8X4),
+                lhsT_scale=w3_scales[:, c * P : (c + 1) * P],
+                rhs=a2_codes[:].bitcast(FP8X4),
+                rhs_scale=a2_scales[:],
+                start=True,
+                stop=True,
+            )
+            bent = held([P, P2], F32, f"bent{c}")
+            lead = held([P, P2], F32, f"lead{c}")
+            nc.scalar.activation(bent[:], y[:], ACT.Tanh)
+            nc.vector.tensor_scalar(lead[:], bent[:], gain_t[:, c : c + 1], None, ALU.mult)
+            queue = nc.sync if c % 2 == 0 else nc.scalar
+            queue.dma_start(out=out[c * P : (c + 1) * P, :], in_=lead[:])

@@ -65,9 +65,9 @@ def tile_list_shell_company_leads_kernel(
         nc.gpsimd.tensor_scalar(shift[:], ones[:], -math.pi / 8, 0.0, ALU.mult, ALU.add)
 
         def load_table(a):
-            nc.sync.dma_start(
-                out=table[a][:].bitcast(I32), in_=tab_words[a].rearrange("p t i -> p (t i)").bitcast(I32)
-            )
+            words = tab_words[a].rearrange("p t i -> p (t i)").bitcast(I32)
+            for c0 in range(0, T, T // 2):
+                nc.sync.dma_start(out=table[a][:, c0 : c0 + T // 2].bitcast(I32), in_=words[:, c0 : c0 + T // 2])
 
         def load_w2(a):
             rows = w2[a * P * PACK : (a + 1) * P * PACK, :]
@@ -78,27 +78,12 @@ def tile_list_shell_company_leads_kernel(
             out=scale_rows[first_row:P, :].bitcast(I32),
             in_=tab_scales.bitcast(I32).rearrange("a q t -> q a t"),
         )
-        nc.sync.dma_start(pos1_t[:], pos1)
-        nc.sync.dma_start(pos2_t[:], pos2)
-        nc.sync.dma_start(pos4_t[:], pos4)
-        nc.sync.dma_start(pos3_t[:], pos3)
         for Q in range(4):
             nc.gpsimd.dma_start(
                 out=w1_scales_raw[32 * Q : 32 * Q + 4, :].bitcast(I32).rearrange("r (a c) -> r a c", a=PASSES),
                 in_=w1_scales.bitcast(I32)[:, 4 * Q : 4 * Q + 4, :].rearrange("a r c -> r a c"),
             )
-        with nc.allow_non_contiguous_dma(reason="one gain value a partition"):
-            nc.gpsimd.dma_start(out=gain_t[:], in_=gain.rearrange("(c p) -> p c", p=P))
-        nc.sync.dma_start(
-            out=w1_raw[:].bitcast(I32).rearrange("p (a c) -> p a c", a=PASSES),
-            in_=w1_words.bitcast(I32).rearrange("a p c -> p a c"),
-        )
         load_table(0)
-        load_table(1)
-        load_w2(0)
-        load_table(2)
-        load_w2(1)
-        load_w2(2)
 
         nc.vector.tensor_copy(picked_rows[:], scale_rows[:].indirect(offs_t[:]))
         for Q in range(4):
@@ -111,10 +96,22 @@ def tile_list_shell_company_leads_kernel(
             out=w1_scales_t[:].bitcast(I32).rearrange("p (a t g w) -> p a t g w", a=PASSES, t=PACK, g=BLOCKS),
             in_=w1_scales_raw[:].bitcast(I32).rearrange("p (a g t w) -> p a t g w", a=PASSES, t=PACK, g=BLOCKS),
         )
-        nc.vector.tensor_copy(
-            out=w1_codes[:].bitcast(I32).rearrange("p (a t g w) -> p a t g w", a=PASSES, t=PACK, g=BLOCKS),
-            in_=w1_raw[:].bitcast(I32).rearrange("p (a g t w) -> p a t g w", a=PASSES, t=PACK, g=BLOCKS),
+
+        load_table(1)
+        load_w2(0)
+        load_table(2)
+        load_w2(1)
+        load_w2(2)
+        nc.sync.dma_start(
+            out=w1_raw[:].bitcast(I32).rearrange("p (a c) -> p a c", a=PASSES),
+            in_=w1_words.bitcast(I32).rearrange("a p c -> p a c"),
         )
+        nc.sync.dma_start(pos1_t[:], pos1)
+        nc.sync.dma_start(pos2_t[:], pos2)
+        nc.sync.dma_start(pos4_t[:], pos4)
+        nc.sync.dma_start(pos3_t[:], pos3)
+        with nc.allow_non_contiguous_dma(reason="one gain value a partition"):
+            nc.sync.dma_start(out=gain_t[:], in_=gain.rearrange("(c p) -> p c", p=P))
 
         def gather_words(a):
             for u in range(2):
@@ -133,12 +130,11 @@ def tile_list_shell_company_leads_kernel(
         def quantise_w2(a, t):
             nc.vector.quantize_mx(out=w2_codes[a][t][:].bitcast(FP8X4), scales=w2_scales[a][t][:], in_=w2_bf[a][t][:])
 
-        def prepare_w2(a):
-            for t in range(PACK + 1):
-                if t < PACK:
-                    round_w2(a, t)
-                if t > 0:
-                    quantise_w2(a, t - 1)
+        def prepare_w2(a, tiles):
+            for t in tiles:
+                round_w2(a, t)
+            for t in tiles:
+                quantise_w2(a, t)
 
         banks = {}
 
@@ -173,21 +169,24 @@ def tile_list_shell_company_leads_kernel(
 
         h = [held([P, S], F32, f"h{t}") for t in range(PACK)]
         a1 = [held([P, P1], F32, f"a1_{t}") for t in range(PACK)]
-        a2 = held([P, PACK, P2], F32, "a2")
+        work = held([P, PACK * S], F32, "work")
+        c2_first = held([P, S], F32, "c2_first")
 
         def gate(t):
-            s = [ring.tile([P, HALF], F32, name=f"s{u}") for u in range(2)]
-            q = [ring.tile([P, HALF], F32, name=f"q{u}") for u in range(2)]
-            c2 = [ring.tile([P, HALF], F32, name=f"c2_{u}") for u in range(2)]
+            s = ring.tile([P, S], F32, name="s")
+            q = ring.tile([P, S], F32, name="q", align_bytes=64)
+            c2 = c2_first[:] if t == 0 else work[:, (t - 1) * S : t * S]
+            halves = [slice(u * HALF, (u + 1) * HALF) for u in range(2)]
+            pieces = halves if t == 0 else [slice(0, S)]
             for u in range(2):
-                nc.scalar.activation(s[u][:], banks["b", t, u][:], ACT.Sin, bias=shift[:], scale=0.25)
-            for u in range(2):
-                nc.scalar.activation(q[u][:], s[u][:], ACT.Square)
-            for u in range(2):
-                nc.scalar.activation(c2[u][:], q[u][:], ACT.Square, bias=ones[:], scale=-2.0)
+                nc.scalar.activation(s[:, halves[u]], banks["b", t, u][:], ACT.Sin, bias=shift[:], scale=0.25)
+            for cols in pieces:
+                nc.scalar.activation(q[:, cols], s[:, cols], ACT.Square)
+            for cols in pieces:
+                nc.scalar.activation(c2[:, cols], q[:, cols], ACT.Square, bias=ones[:], scale=-2.0)
             for u in range(2):
                 nc.vector.scalar_tensor_tensor(
-                    h[t][:, u * HALF : (u + 1) * HALF], c2[u][:], 2.0, banks["f", t, u][:], ALU.mult, ALU.mult
+                    h[t][:, halves[u]], c2[:, halves[u]], 2.0, banks["f", t, u][:], ALU.mult, ALU.mult
                 )
 
         def pairs(t):
@@ -200,30 +199,41 @@ def tile_list_shell_company_leads_kernel(
             nc.vector.tensor_tensor(a1[t][:], g1[:], g2[:], ALU.max)
             return g4
 
-        def differences(t, g4):
-            nc.vector.tensor_tensor(a2[:, t, :], a1[t][:].indirect(pos3_t[:]), g4[:], ALU.subtract)
+        def differences(t, g4, pieces):
+            width = P2 // pieces
+            for j0 in range(0, P2, width):
+                picked = a1[t][:].indirect(pos3_t[:, j0 // 16 : (j0 + width) // 16])
+                a2_cols = work[:, t * S + j0 : t * S + j0 + width]
+                nc.vector.tensor_tensor(a2_cols, picked, g4[:, j0 : j0 + width], ALU.subtract)
 
         open_banks(0)
         open_banks(1)
         gather_words(0)
-        products("f", (0, 1), 0)
         w3_raw = held([P, PACK, N], F32, "table0")
         for t in range(PACK):
             nc.sync.dma_start(
                 out=w3_raw[:, t, :], in_=w3.rearrange("(g t i) n -> t g i n", t=PACK, i=RUN)[t]
             )
         gather_words(1)
-        products("f", (0, 1), 1)
-        prepare_w2(0)
+        prepare_w2(0, (0, 1))
         products("b", (0, 1), 0)
+        prepare_w2(0, (2, 3))
         gather_words(2)
-        products("f", (0, 1), 2)
-        prepare_w2(1)
+        prepare_w2(1, (0, 1))
         products("b", (0, 1), 1)
-        prepare_w2(2)
-        products("b", (0, 1), 2)
+        prepare_w2(2, (0, 1))
+        nc.vector.tensor_copy(
+            out=w1_codes[:].bitcast(I32).rearrange("p (a t g w) -> p a t g w", a=PASSES, t=PACK, g=BLOCKS),
+            in_=w1_raw[:].bitcast(I32).rearrange("p (a g t w) -> p a t g w", a=PASSES, t=PACK, g=BLOCKS),
+        )
+        for t in (0, 1):
+            products("b", (t,), 2)
+            for u in range(2):
+                for a in range(PASSES):
+                    product("f", t, u, a)
+        prepare_w2(1, (2, 3))
+        prepare_w2(2, (2, 3))
 
-        w3_bf = held([P, N * PACK], BF16, "w3_bf")
         w3_codes = held([P, N], U32, "w3_codes")
         w3_scales = held([P, N], U8, "w3_scales")
 
@@ -236,39 +246,44 @@ def tile_list_shell_company_leads_kernel(
                     for a in range(PASSES):
                         products(kind, (t + 2,), a)
             if t > 0:
-                differences(t - 1, memo[t - 1])
+                differences(t - 1, memo[t - 1], 1)
             if t == PACK - 1:
+                w3_bf = ring.tile([P, N * PACK], BF16, name="q", align_bytes=64)
                 nc.scalar.copy(
                     out=w3_bf[:].rearrange("p (c l j) -> p c j l", l=4, j=PACK),
                     in_=w3_raw[:].rearrange("p j (c l) -> p c j l", l=4),
                 )
             memo[t] = pairs(t)
         nc.vector.quantize_mx(out=w3_codes[:].bitcast(FP8X4), scales=w3_scales[:], in_=w3_bf[:])
-        differences(PACK - 1, memo[PACK - 1])
+        differences(PACK - 1, memo[PACK - 1], 2)
 
-        a2_bf = held([P, P2 * PACK], BF16, "a2_bf")
-        a2_codes = held([P, P2], U32, "a2_codes")
-        a2_scales = held([P, P2], U8, "a2_scales")
-        nc.vector.tensor_copy(
-            out=a2_bf[:].rearrange("p (c l j) -> p c j l", l=4, j=PACK),
-            in_=a2[:].rearrange("p j (c l) -> p c j l", l=4),
-        )
-        nc.vector.quantize_mx(out=a2_codes[:].bitcast(FP8X4), scales=a2_scales[:], in_=a2_bf[:])
-
-        for c, tag in enumerate(("b0", "b1", "f0", "f1")):
-            y = psum.tile([P, P2], F32, name=f"y{c}", tag=tag)
-            nc.tensor.matmul_mx(
-                out=y[:],
-                lhsT=w3_codes[:, c * P : (c + 1) * P].bitcast(FP8X4),
-                lhsT_scale=w3_scales[:, c * P : (c + 1) * P],
-                rhs=a2_codes[:].bitcast(FP8X4),
-                rhs_scale=a2_scales[:],
-                start=True,
-                stop=True,
+        a2_bf = [held([P, P * PACK], BF16, f"a2_bf{u}") for u in range(2)]
+        a2_codes = [held([P, P], U32, f"a2_codes{u}") for u in range(2)]
+        a2_scales = [held([P, P], U8, f"a2_scales{u}") for u in range(2)]
+        a2 = work[:].rearrange("p (j c l) -> p c j l", j=PACK, l=4)
+        for u in range(2):
+            nc.vector.tensor_copy(
+                out=a2_bf[u][:].rearrange("p (c l j) -> p c j l", l=4, j=PACK),
+                in_=a2[:, u * P // 4 : (u + 1) * P // 4],
             )
+        for u in range(2):
+            nc.vector.quantize_mx(out=a2_codes[u][:].bitcast(FP8X4), scales=a2_scales[u][:], in_=a2_bf[u][:])
+
+        y = [psum.tile([P, P2], F32, name=f"y{c}", tag=tag) for c, tag in enumerate(("b0", "b1", "f0", "f1"))]
+        for u in range(2):
+            for c in range(PACK):
+                nc.tensor.matmul_mx(
+                    out=y[c][:, u * P : (u + 1) * P],
+                    lhsT=w3_codes[:, c * P : (c + 1) * P].bitcast(FP8X4),
+                    lhsT_scale=w3_scales[:, c * P : (c + 1) * P],
+                    rhs=a2_codes[u][:].bitcast(FP8X4),
+                    rhs_scale=a2_scales[u][:],
+                    start=True,
+                    stop=True,
+                )
+        for c in range(PACK):
             bent = held([P, P2], F32, f"bent{c}")
             lead = held([P, P2], F32, f"lead{c}")
-            nc.scalar.activation(bent[:], y[:], ACT.Tanh)
+            nc.scalar.activation(bent[:], y[c][:], ACT.Tanh)
             nc.vector.tensor_scalar(lead[:], bent[:], gain_t[:, c : c + 1], None, ALU.mult)
-            queue = nc.sync if c % 2 == 0 else nc.scalar
-            queue.dma_start(out=out[c * P : (c + 1) * P, :], in_=lead[:])
+            nc.sync.dma_start(out=out[c * P : (c + 1) * P, :], in_=lead[:])

@@ -21,6 +21,9 @@ P = 128
 PACK = 4
 PASSES = K // (P * PACK)
 HALF = 512
+QUARTER = 256
+ASIN_PI_8 = 0.40356460692486534
+assert abs(math.sin(ASIN_PI_8) - math.pi / 8) < 1e-15
 BLOCKS = 16
 RUN = 8
 
@@ -47,7 +50,6 @@ def tile_list_shell_company_leads_kernel(
         picked_rows = held([P, S], U8, "picked_rows")
         v_scales = held([P, PASSES * S], U8, "v_scales")
         w1_scales_raw = held([P, PASSES * H], U8, "w1_scales_raw")
-        w1_scales_t = held([P, PASSES * H], U8, "w1_scales_t")
         w1_raw = held([P, PASSES * 2 * H], U8, "w1_raw")
         w1_codes = held([P, PASSES * 2 * H], U8, "w1_codes")
         table = [held([P, T], U32, f"table{a}") for a in range(PASSES)]
@@ -59,19 +61,20 @@ def tile_list_shell_company_leads_kernel(
         shift = held([P, 1], F32, "shift")
 
         nc.vector.memset(scale_rows[0:first_row, :].bitcast(I32), 0)
+        nc.gpsimd.memset(ones[:], 1.0)
         nc.gpsimd.memset(w1_scales_raw[:].bitcast(I32), 0)
         nc.gpsimd.memset(v_scales[:].bitcast(I32), 0)
-        nc.gpsimd.memset(ones[:], 1.0)
-        nc.gpsimd.tensor_scalar(shift[:], ones[:], -math.pi / 8, 0.0, ALU.mult, ALU.add)
+        nc.scalar.activation(shift[:], ones[:], ACT.Sin, scale=-ASIN_PI_8)
 
         def load_table(a):
             words = tab_words[a].rearrange("p t i -> p (t i)").bitcast(I32)
             for c0 in range(0, T, T // 2):
                 nc.sync.dma_start(out=table[a][:, c0 : c0 + T // 2].bitcast(I32), in_=words[:, c0 : c0 + T // 2])
 
-        def load_w2(a):
-            rows = w2[a * P * PACK : (a + 1) * P * PACK, :]
-            nc.sync.dma_start(out=w2_raw[a][:], in_=rows.rearrange("(p j) c -> p j c", j=PACK))
+        def load_w2(a, width=H):
+            rows = w2[a * P * PACK : (a + 1) * P * PACK, :].rearrange("(p j) c -> p j c", j=PACK)
+            for c0 in range(0, H, width):
+                nc.sync.dma_start(out=w2_raw[a][:, :, c0 : c0 + width], in_=rows[:, :, c0 : c0 + width])
 
         nc.sync.dma_start(offs_t[:], offs)
         nc.sync.dma_start(
@@ -92,16 +95,11 @@ def tile_list_shell_company_leads_kernel(
                 in_=picked_rows[first_row + 12 * Q : first_row + 12 * Q + 12, :].bitcast(I32),
             )
 
-        nc.vector.tensor_copy(
-            out=w1_scales_t[:].bitcast(I32).rearrange("p (a t g w) -> p a t g w", a=PASSES, t=PACK, g=BLOCKS),
-            in_=w1_scales_raw[:].bitcast(I32).rearrange("p (a g t w) -> p a t g w", a=PASSES, t=PACK, g=BLOCKS),
-        )
-
         load_table(1)
         load_w2(0)
         load_table(2)
         load_w2(1)
-        load_w2(2)
+        load_w2(2, H // 2)
         nc.sync.dma_start(
             out=w1_raw[:].bitcast(I32).rearrange("p (a c) -> p a c", a=PASSES),
             in_=w1_words.bitcast(I32).rearrange("a p c -> p a c"),
@@ -122,50 +120,48 @@ def tile_list_shell_company_leads_kernel(
         w2_codes = [[held([P, P], U32, f"w2_codes{a}_{t}") for t in range(PACK)] for a in range(PASSES)]
         w2_scales = [[held([P, P], U8, f"w2_scales{a}_{t}") for t in range(PACK)] for a in range(PASSES)]
 
-        def round_w2(a, t):
+        def round_w2(a, t, copy, blocks=slice(0, BLOCKS)):
             src = w2_raw[a][:].rearrange("p j (g t h l) -> p t g h j l", t=PACK, h=2, l=4)[:, t]
             dst = w2_bf[a][t][:].rearrange("p (g h l j) -> p g h j l", h=2, l=4, j=PACK)
-            nc.vector.tensor_copy(out=dst, in_=src)
+            copy(out=dst[:, blocks], in_=src[:, blocks])
 
         def quantise_w2(a, t):
             nc.vector.quantize_mx(out=w2_codes[a][t][:].bitcast(FP8X4), scales=w2_scales[a][t][:], in_=w2_bf[a][t][:])
 
-        def prepare_w2(a, tiles):
+        def prepare_w2(a, tiles, copy):
             for t in tiles:
-                round_w2(a, t)
+                round_w2(a, t, copy)
             for t in tiles:
                 quantise_w2(a, t)
 
         banks = {}
 
-        def open_banks(t):
-            for u in range(2):
-                banks["f", t, u] = psum.tile([P, HALF], F32, name=f"f{t}_{u}", tag=f"f{u}")
-                banks["b", t, u] = psum.tile([P, HALF], F32, name=f"b{t}_{u}", tag=f"b{u}")
+        def piece_width(kind, t):
+            return QUARTER if (kind, t) == ("b", 0) else HALF
 
-        def product(kind, t, u, a):
-            if kind == "f":
-                c0 = a * H + t * P
-                lhsT = w1_codes[:, 2 * c0 : 2 * (c0 + P)].bitcast(FP4X4)
-                lhsT_scale = w1_scales_t[:, c0 : c0 + P]
-            else:
-                lhsT = w2_codes[a][t][:].bitcast(FP8X4)
-                lhsT_scale = w2_scales[a][t][:]
-            s0 = a * S + u * HALF
-            nc.tensor.matmul_mx(
-                out=banks[kind, t, u][:],
-                lhsT=lhsT,
-                lhsT_scale=lhsT_scale,
-                rhs=v_codes[a][u][:].bitcast(FP8X4),
-                rhs_scale=v_scales[:, s0 : s0 + HALF],
-                start=(a == 0),
-                stop=(a == PASSES - 1),
-            )
-
-        def products(kind, tiles, a):
-            for t in tiles:
-                for u in range(2):
-                    product(kind, t, u, a)
+        def products(kind, t):
+            width = piece_width(kind, t)
+            for n, j0 in enumerate(range(0, S, width)):
+                bank = psum.tile([P, width], F32, name=f"{kind}{t}_{n}", tag=f"{kind}{n % 2}")
+                banks[kind, t, j0] = bank
+                u, c1 = divmod(j0, HALF)
+                for a in range(PASSES):
+                    if kind == "f":
+                        c0 = a * H + t * P
+                        lhsT = w1_codes[:, 2 * c0 : 2 * (c0 + P)].bitcast(FP4X4)
+                        lhsT_scale = w1_scales_t[:, c0 : c0 + P]
+                    else:
+                        lhsT = w2_codes[a][t][:].bitcast(FP8X4)
+                        lhsT_scale = w2_scales[a][t][:]
+                    nc.tensor.matmul_mx(
+                        out=bank[:],
+                        lhsT=lhsT,
+                        lhsT_scale=lhsT_scale,
+                        rhs=v_codes[a][u][:, c1 : c1 + width].bitcast(FP8X4),
+                        rhs_scale=v_scales[:, a * S + j0 : a * S + j0 + width],
+                        start=(a == 0),
+                        stop=(a == PASSES - 1),
+                    )
 
         h = [held([P, S], F32, f"h{t}") for t in range(PACK)]
         a1 = [held([P, P1], F32, f"a1_{t}") for t in range(PACK)]
@@ -176,17 +172,24 @@ def tile_list_shell_company_leads_kernel(
             s = ring.tile([P, S], F32, name="s")
             q = ring.tile([P, S], F32, name="q", align_bytes=64)
             c2 = c2_first[:] if t == 0 else work[:, (t - 1) * S : t * S]
-            halves = [slice(u * HALF, (u + 1) * HALF) for u in range(2)]
-            pieces = halves if t == 0 else [slice(0, S)]
-            for u in range(2):
-                nc.scalar.activation(s[:, halves[u]], banks["b", t, u][:], ACT.Sin, bias=shift[:], scale=0.25)
-            for cols in pieces:
-                nc.scalar.activation(q[:, cols], s[:, cols], ACT.Square)
-            for cols in pieces:
-                nc.scalar.activation(c2[:, cols], q[:, cols], ACT.Square, bias=ones[:], scale=-2.0)
-            for u in range(2):
+            width = piece_width("b", t)
+            span = width if t == 0 else S
+            for j0 in range(0, S, width):
+                cols = slice(j0, j0 + width)
+                nc.scalar.activation(s[:, cols], banks["b", t, j0][:], ACT.Sin, bias=shift[:], scale=0.25)
+                if (j0 + width) % span == 0:
+                    cols = slice(j0 + width - span, j0 + width)
+                    nc.scalar.activation(q[:, cols], s[:, cols], ACT.Square)
+                    nc.scalar.activation(c2[:, cols], q[:, cols], ACT.Square, bias=ones[:], scale=-2.0)
+            for j0 in range(0, S, width):
+                f_bank = banks["f", t, j0 - j0 % HALF]
                 nc.vector.scalar_tensor_tensor(
-                    h[t][:, halves[u]], c2[:, halves[u]], 2.0, banks["f", t, u][:], ALU.mult, ALU.mult
+                    h[t][:, j0 : j0 + width],
+                    c2[:, j0 : j0 + width],
+                    2.0,
+                    f_bank[:, j0 % HALF : j0 % HALF + width],
+                    ALU.mult,
+                    ALU.mult,
                 )
 
         def pairs(t):
@@ -206,8 +209,6 @@ def tile_list_shell_company_leads_kernel(
                 a2_cols = work[:, t * S + j0 : t * S + j0 + width]
                 nc.vector.tensor_tensor(a2_cols, picked, g4[:, j0 : j0 + width], ALU.subtract)
 
-        open_banks(0)
-        open_banks(1)
         gather_words(0)
         w3_raw = held([P, PACK, N], F32, "table0")
         for t in range(PACK):
@@ -215,24 +216,28 @@ def tile_list_shell_company_leads_kernel(
                 out=w3_raw[:, t, :], in_=w3.rearrange("(g t i) n -> t g i n", t=PACK, i=RUN)[t]
             )
         gather_words(1)
-        prepare_w2(0, (0, 1))
-        products("b", (0, 1), 0)
-        prepare_w2(0, (2, 3))
+        prepare_w2(0, range(PACK), nc.vector.tensor_copy)
+        w1_scales_t = held([P, PASSES * H], U8, "w2_raw0")
+        nc.vector.tensor_copy(
+            out=w1_scales_t[:].bitcast(I32).rearrange("p (a t g w) -> p a t g w", a=PASSES, t=PACK, g=BLOCKS),
+            in_=w1_scales_raw[:].bitcast(I32).rearrange("p (a g t w) -> p a t g w", a=PASSES, t=PACK, g=BLOCKS),
+        )
+
         gather_words(2)
-        prepare_w2(1, (0, 1))
-        products("b", (0, 1), 1)
-        prepare_w2(2, (0, 1))
+        prepare_w2(1, (0, 1), nc.vector.tensor_copy)
+        prepare_w2(1, (2, 3), nc.scalar.copy)
+        for g0 in range(0, BLOCKS, BLOCKS // 2):
+            round_w2(2, 0, nc.vector.tensor_copy, slice(g0, g0 + BLOCKS // 2))
+        quantise_w2(2, 0)
+        prepare_w2(2, (1,), nc.scalar.copy)
         nc.vector.tensor_copy(
             out=w1_codes[:].bitcast(I32).rearrange("p (a t g w) -> p a t g w", a=PASSES, t=PACK, g=BLOCKS),
             in_=w1_raw[:].bitcast(I32).rearrange("p (a g t w) -> p a t g w", a=PASSES, t=PACK, g=BLOCKS),
         )
+        prepare_w2(2, (2, 3), nc.vector.tensor_copy)
         for t in (0, 1):
-            products("b", (t,), 2)
-            for u in range(2):
-                for a in range(PASSES):
-                    product("f", t, u, a)
-        prepare_w2(1, (2, 3))
-        prepare_w2(2, (2, 3))
+            products("b", t)
+            products("f", t)
 
         w3_codes = held([P, N], U32, "w3_codes")
         w3_scales = held([P, N], U8, "w3_scales")
@@ -241,10 +246,8 @@ def tile_list_shell_company_leads_kernel(
         for t in range(PACK):
             gate(t)
             if t + 2 < PACK:
-                open_banks(t + 2)
-                for kind in ("b", "f"):
-                    for a in range(PASSES):
-                        products(kind, (t + 2,), a)
+                products("b", t + 2)
+                products("f", t + 2)
             if t > 0:
                 differences(t - 1, memo[t - 1], 1)
             if t == PACK - 1:

@@ -20,12 +20,14 @@ ALU = mybir.AluOpType
 P = 128
 PACK = 4
 PASSES = K // (P * PACK)
+BLOCKS = 16
+RUN = 8
+LIST_ROWS = 16
+LINE = 4
 HALF = 512
 QUARTER = 256
 ASIN_PI_8 = 0.40356460692486534
 assert abs(math.sin(ASIN_PI_8) - math.pi / 8) < 1e-15
-BLOCKS = 16
-RUN = 8
 
 
 def tile_list_shell_company_leads_kernel(
@@ -40,11 +42,11 @@ def tile_list_shell_company_leads_kernel(
         def held(shape, dtype, name):
             return keep.tile(shape, dtype, name=name, align_bytes=64)
 
-        offs_t = held([P, S // 16], U16, "offs_t")
-        pos1_t = held([P, P1 // 16], U16, "pos1_t")
-        pos2_t = held([P, P1 // 16], U16, "pos2_t")
-        pos3_t = held([P, P2 // 16], U16, "pos3_t")
-        pos4_t = held([P, P2 // 16], U16, "pos4_t")
+        offs_t = held([P, S // LIST_ROWS], U16, "offs_t")
+        pos1_t = held([P, P1 // LIST_ROWS], U16, "pos1_t")
+        pos2_t = held([P, P1 // LIST_ROWS], U16, "pos2_t")
+        pos3_t = held([P, P2 // LIST_ROWS], U16, "pos3_t")
+        pos4_t = held([P, P2 // LIST_ROWS], U16, "pos4_t")
 
         scale_rows = held([P, T], U8, "scale_rows")
         picked_rows = held([P, S], U8, "picked_rows")
@@ -53,13 +55,13 @@ def tile_list_shell_company_leads_kernel(
         w1_raw = held([P, PASSES * 2 * H], U8, "w1_raw")
         w1_codes = held([P, PASSES * 2 * H], U8, "w1_codes")
         table = [held([P, T], U32, f"table{a}") for a in range(PASSES)]
-        first_row = P - 16 * PASSES
         v_codes = [[held([P, HALF], U32, f"v_codes{a}_{u}") for u in range(2)] for a in range(PASSES)]
         w2_raw = [held([P, PACK, H], F32, f"w2_raw{a}") for a in range(PASSES)]
         gain_t = held([P, PACK], F32, "gain_t")
         ones = held([P, 1], F32, "ones")
         shift = held([P, 1], F32, "shift")
 
+        first_row = P - BLOCKS * PASSES
         nc.vector.memset(scale_rows[0:first_row, :].bitcast(I32), 0)
         nc.gpsimd.memset(ones[:], 1.0)
         nc.gpsimd.memset(w1_scales_raw[:].bitcast(I32), 0)
@@ -76,23 +78,27 @@ def tile_list_shell_company_leads_kernel(
             for c0 in range(0, H, width):
                 nc.sync.dma_start(out=w2_raw[a][:, :, c0 : c0 + width], in_=rows[:, :, c0 : c0 + width])
 
+        def plane_rows(planes, quadrant):
+            rows = planes[32 * quadrant : 32 * quadrant + 4, :]
+            return rows.bitcast(I32).rearrange("r (a c) -> r a c", a=PASSES)
+
         nc.sync.dma_start(offs_t[:], offs)
         nc.sync.dma_start(
             out=scale_rows[first_row:P, :].bitcast(I32),
             in_=tab_scales.bitcast(I32).rearrange("a q t -> q a t"),
         )
-        for Q in range(4):
+        for quadrant in range(4):
             nc.gpsimd.dma_start(
-                out=w1_scales_raw[32 * Q : 32 * Q + 4, :].bitcast(I32).rearrange("r (a c) -> r a c", a=PASSES),
-                in_=w1_scales.bitcast(I32)[:, 4 * Q : 4 * Q + 4, :].rearrange("a r c -> r a c"),
+                out=plane_rows(w1_scales_raw, quadrant),
+                in_=w1_scales.bitcast(I32)[:, 4 * quadrant : 4 * quadrant + 4, :].rearrange("a r c -> r a c"),
             )
         load_table(0)
 
         nc.vector.tensor_copy(picked_rows[:], scale_rows[:].indirect(offs_t[:]))
-        for Q in range(4):
+        for quadrant in range(4):
+            row0 = first_row + 4 * PASSES * quadrant
             nc.scalar.dma_start(
-                out=v_scales[32 * Q : 32 * Q + 4, :].bitcast(I32).rearrange("r (a c) -> r a c", a=PASSES),
-                in_=picked_rows[first_row + 12 * Q : first_row + 12 * Q + 12, :].bitcast(I32),
+                out=plane_rows(v_scales, quadrant), in_=picked_rows[row0 : row0 + 4 * PASSES, :].bitcast(I32)
             )
 
         load_table(1)
@@ -113,7 +119,7 @@ def tile_list_shell_company_leads_kernel(
 
         def gather_words(a):
             for u in range(2):
-                cols = slice(u * HALF // 16, (u + 1) * HALF // 16)
+                cols = slice(u * HALF // LIST_ROWS, (u + 1) * HALF // LIST_ROWS)
                 nc.vector.tensor_copy(v_codes[a][u][:], table[a][:].indirect(offs_t[:, cols]))
 
         w2_bf = [[held([P, P * PACK], BF16, f"w2_bf{a}_{t}") for t in range(PACK)] for a in range(PASSES)]
@@ -121,8 +127,8 @@ def tile_list_shell_company_leads_kernel(
         w2_scales = [[held([P, P], U8, f"w2_scales{a}_{t}") for t in range(PACK)] for a in range(PASSES)]
 
         def round_w2(a, t, copy, blocks=slice(0, BLOCKS)):
-            src = w2_raw[a][:].rearrange("p j (g t h l) -> p t g h j l", t=PACK, h=2, l=4)[:, t]
-            dst = w2_bf[a][t][:].rearrange("p (g h l j) -> p g h j l", h=2, l=4, j=PACK)
+            src = w2_raw[a][:].rearrange("p j (g t h l) -> p t g h j l", t=PACK, h=RUN // LINE, l=LINE)[:, t]
+            dst = w2_bf[a][t][:].rearrange("p (g h l j) -> p g h j l", h=RUN // LINE, l=LINE, j=PACK)
             copy(out=dst[:, blocks], in_=src[:, blocks])
 
         def quantise_w2(a, t):
@@ -166,26 +172,26 @@ def tile_list_shell_company_leads_kernel(
         h = [held([P, S], F32, f"h{t}") for t in range(PACK)]
         a1 = [held([P, P1], F32, f"a1_{t}") for t in range(PACK)]
         work = held([P, PACK * S], F32, "work")
-        c2_first = held([P, S], F32, "c2_first")
+        cos2_first = held([P, S], F32, "cos2_first")
 
         def gate(t):
-            s = ring.tile([P, S], F32, name="s")
-            q = ring.tile([P, S], F32, name="q", align_bytes=64)
-            c2 = c2_first[:] if t == 0 else work[:, (t - 1) * S : t * S]
+            sine = ring.tile([P, S], F32, name="sine")
+            square = ring.tile([P, S], F32, name="square", align_bytes=64)
+            cos2 = cos2_first[:] if t == 0 else work[:, (t - 1) * S : t * S]
             width = piece_width("b", t)
             span = width if t == 0 else S
             for j0 in range(0, S, width):
                 cols = slice(j0, j0 + width)
-                nc.scalar.activation(s[:, cols], banks["b", t, j0][:], ACT.Sin, bias=shift[:], scale=0.25)
+                nc.scalar.activation(sine[:, cols], banks["b", t, j0][:], ACT.Sin, bias=shift[:], scale=0.25)
                 if (j0 + width) % span == 0:
-                    cols = slice(j0 + width - span, j0 + width)
-                    nc.scalar.activation(q[:, cols], s[:, cols], ACT.Square)
-                    nc.scalar.activation(c2[:, cols], q[:, cols], ACT.Square, bias=ones[:], scale=-2.0)
+                    done = slice(j0 + width - span, j0 + width)
+                    nc.scalar.activation(square[:, done], sine[:, done], ACT.Square)
+                    nc.scalar.activation(cos2[:, done], square[:, done], ACT.Square, bias=ones[:], scale=-2.0)
             for j0 in range(0, S, width):
                 f_bank = banks["f", t, j0 - j0 % HALF]
                 nc.vector.scalar_tensor_tensor(
                     h[t][:, j0 : j0 + width],
-                    c2[:, j0 : j0 + width],
+                    cos2[:, j0 : j0 + width],
                     2.0,
                     f_bank[:, j0 % HALF : j0 % HALF + width],
                     ALU.mult,
@@ -193,28 +199,26 @@ def tile_list_shell_company_leads_kernel(
                 )
 
         def pairs(t):
-            g1 = ring.tile([P, P1], F32, name="g1")
-            g2 = ring.tile([P, P1], F32, name="g2")
-            g4 = ring.tile([P, P2], F32, name="g4")
-            nc.vector.tensor_copy(g1[:], h[t][:].indirect(pos1_t[:]))
-            nc.vector.tensor_copy(g2[:], h[t][:].indirect(pos2_t[:]))
-            nc.vector.tensor_copy(g4[:], h[t][:].indirect(pos4_t[:]))
-            nc.vector.tensor_tensor(a1[t][:], g1[:], g2[:], ALU.max)
-            return g4
+            first = ring.tile([P, P1], F32, name="first")
+            second = ring.tile([P, P1], F32, name="second")
+            memo = ring.tile([P, P2], F32, name="memo")
+            nc.vector.tensor_copy(first[:], h[t][:].indirect(pos1_t[:]))
+            nc.vector.tensor_copy(second[:], h[t][:].indirect(pos2_t[:]))
+            nc.vector.tensor_copy(memo[:], h[t][:].indirect(pos4_t[:]))
+            nc.vector.tensor_tensor(a1[t][:], first[:], second[:], ALU.max)
+            return memo
 
-        def differences(t, g4, pieces):
+        def differences(t, memo, pieces):
             width = P2 // pieces
             for j0 in range(0, P2, width):
-                picked = a1[t][:].indirect(pos3_t[:, j0 // 16 : (j0 + width) // 16])
+                picked = a1[t][:].indirect(pos3_t[:, j0 // LIST_ROWS : (j0 + width) // LIST_ROWS])
                 a2_cols = work[:, t * S + j0 : t * S + j0 + width]
-                nc.vector.tensor_tensor(a2_cols, picked, g4[:, j0 : j0 + width], ALU.subtract)
+                nc.vector.tensor_tensor(a2_cols, picked, memo[:, j0 : j0 + width], ALU.subtract)
 
         gather_words(0)
         w3_raw = held([P, PACK, N], F32, "table0")
         for t in range(PACK):
-            nc.sync.dma_start(
-                out=w3_raw[:, t, :], in_=w3.rearrange("(g t i) n -> t g i n", t=PACK, i=RUN)[t]
-            )
+            nc.sync.dma_start(out=w3_raw[:, t, :], in_=w3.rearrange("(g t i) n -> t g i n", t=PACK, i=RUN)[t])
         gather_words(1)
         prepare_w2(0, range(PACK), nc.vector.tensor_copy)
         w1_scales_t = held([P, PASSES * H], U8, "w2_raw0")
@@ -222,7 +226,6 @@ def tile_list_shell_company_leads_kernel(
             out=w1_scales_t[:].bitcast(I32).rearrange("p (a t g w) -> p a t g w", a=PASSES, t=PACK, g=BLOCKS),
             in_=w1_scales_raw[:].bitcast(I32).rearrange("p (a g t w) -> p a t g w", a=PASSES, t=PACK, g=BLOCKS),
         )
-
         gather_words(2)
         prepare_w2(1, (0, 1), nc.vector.tensor_copy)
         prepare_w2(1, (2, 3), nc.scalar.copy)
@@ -242,41 +245,45 @@ def tile_list_shell_company_leads_kernel(
         w3_codes = held([P, N], U32, "w3_codes")
         w3_scales = held([P, N], U8, "w3_scales")
 
-        memo = {}
+        memos = {}
         for t in range(PACK):
             gate(t)
             if t + 2 < PACK:
                 products("b", t + 2)
                 products("f", t + 2)
             if t > 0:
-                differences(t - 1, memo[t - 1], 1)
+                differences(t - 1, memos[t - 1], 1)
             if t == PACK - 1:
-                w3_bf = ring.tile([P, N * PACK], BF16, name="q", align_bytes=64)
+                w3_bf = ring.tile([P, N * PACK], BF16, name="square", align_bytes=64)
                 nc.scalar.copy(
-                    out=w3_bf[:].rearrange("p (c l j) -> p c j l", l=4, j=PACK),
-                    in_=w3_raw[:].rearrange("p j (c l) -> p c j l", l=4),
+                    out=w3_bf[:].rearrange("p (c l j) -> p c j l", l=LINE, j=PACK),
+                    in_=w3_raw[:].rearrange("p j (c l) -> p c j l", l=LINE),
                 )
-            memo[t] = pairs(t)
+            memos[t] = pairs(t)
         nc.vector.quantize_mx(out=w3_codes[:].bitcast(FP8X4), scales=w3_scales[:], in_=w3_bf[:])
-        differences(PACK - 1, memo[PACK - 1], 2)
 
+        differences(PACK - 1, memos[PACK - 1], 2)
         a2_bf = [held([P, P * PACK], BF16, f"a2_bf{u}") for u in range(2)]
         a2_codes = [held([P, P], U32, f"a2_codes{u}") for u in range(2)]
         a2_scales = [held([P, P], U8, f"a2_scales{u}") for u in range(2)]
-        a2 = work[:].rearrange("p (j c l) -> p c j l", j=PACK, l=4)
+        a2 = work[:].rearrange("p (t c l) -> p c t l", t=PACK, l=LINE)
         for u in range(2):
             nc.vector.tensor_copy(
-                out=a2_bf[u][:].rearrange("p (c l j) -> p c j l", l=4, j=PACK),
-                in_=a2[:, u * P // 4 : (u + 1) * P // 4],
+                out=a2_bf[u][:].rearrange("p (c l t) -> p c t l", l=LINE, t=PACK),
+                in_=a2[:, u * P // LINE : (u + 1) * P // LINE],
             )
         for u in range(2):
             nc.vector.quantize_mx(out=a2_codes[u][:].bitcast(FP8X4), scales=a2_scales[u][:], in_=a2_bf[u][:])
 
-        y = [psum.tile([P, P2], F32, name=f"y{c}", tag=tag) for c, tag in enumerate(("b0", "b1", "f0", "f1"))]
-        for u in range(2):
-            for c in range(PACK):
+        out_view = out.rearrange("(c p) j -> p c j", p=P)
+        groups = [(u, range(c0, c0 + 2)) for u in range(2) for c0 in (0, 2)]
+        for n, ((u, chunks), tag) in enumerate(zip(groups, ("b0", "b1", "f0", "f1"))):
+            y = psum.tile([P, len(chunks), P], F32, name=f"y{n}", tag=tag)
+            bent = held([P, len(chunks), P], F32, f"bent{n}")
+            lead = held([P, len(chunks), P], F32, f"lead{n}")
+            for m, c in enumerate(chunks):
                 nc.tensor.matmul_mx(
-                    out=y[c][:, u * P : (u + 1) * P],
+                    out=y[:, m, :],
                     lhsT=w3_codes[:, c * P : (c + 1) * P].bitcast(FP8X4),
                     lhsT_scale=w3_scales[:, c * P : (c + 1) * P],
                     rhs=a2_codes[u][:].bitcast(FP8X4),
@@ -284,9 +291,7 @@ def tile_list_shell_company_leads_kernel(
                     start=True,
                     stop=True,
                 )
-        for c in range(PACK):
-            bent = held([P, P2], F32, f"bent{c}")
-            lead = held([P, P2], F32, f"lead{c}")
-            nc.scalar.activation(bent[:], y[c][:], ACT.Tanh)
-            nc.vector.tensor_scalar(lead[:], bent[:], gain_t[:, c : c + 1], None, ALU.mult)
-            nc.sync.dma_start(out=out[c * P : (c + 1) * P, :], in_=lead[:])
+            nc.scalar.activation(bent[:], y[:], ACT.Tanh)
+            for m, c in enumerate(chunks):
+                nc.vector.tensor_scalar(lead[:, m, :], bent[:, m, :], gain_t[:, c : c + 1], None, ALU.mult)
+            nc.sync.dma_start(out=out_view[:, chunks.start : chunks.stop, u * P : (u + 1) * P], in_=lead[:])

import math
from contextlib import ExitStack

import concourse.mybir as mybir

K, T, S, P1, P2, H, N = 1536, 4096, 1024, 512, 256, 512, 512
FLOPS = 2 * K * H * S * 2 + 2 * H * N * P2

F32 = mybir.dt.float32
BF16 = mybir.dt.bfloat16
I32 = mybir.dt.int32
U32 = mybir.dt.uint32
U16 = mybir.dt.uint16
U8 = mybir.dt.uint8
FP8X4 = mybir.dt.float8_e4m3fn_x4
FP4X4 = mybir.dt.float4_e2m1fn_x4
ACT = mybir.ActivationFunctionType
ALU = mybir.AluOpType

P = 128
PACK = 4
PASSES = K // (P * PACK)
BLOCKS = 16
RUN = 8
LIST_ROWS = 16
LINE = 4
HALF = 512
QUARTER = 256
ASIN_PI_8 = 0.40356460692486534
assert abs(math.sin(ASIN_PI_8) - math.pi / 8) < 1e-15


def tile_list_shell_company_leads_kernel(
    tc, tab_words, tab_scales, offs, pos1, pos2, pos3, pos4, w1_words, w1_scales, w2, w3, gain, out
):
    nc = tc.nc
    with ExitStack() as ctx:
        keep = ctx.enter_context(tc.tile_pool(name="keep", bufs=1))
        ring = ctx.enter_context(tc.tile_pool(name="ring", bufs=2))
        psum = ctx.enter_context(tc.psum_pool(name="psum", bufs=2))

        def held(shape, dtype, name):
            return keep.tile(shape, dtype, name=name, align_bytes=64)

        offs_t = held([P, S // LIST_ROWS], U16, "offs_t")
        pos1_t = held([P, P1 // LIST_ROWS], U16, "pos1_t")
        pos2_t = held([P, P1 // LIST_ROWS], U16, "pos2_t")
        pos3_t = held([P, P2 // LIST_ROWS], U16, "pos3_t")
        pos4_t = held([P, P2 // LIST_ROWS], U16, "pos4_t")

        scale_rows = held([P, T], U8, "scale_rows")
        picked_rows = held([P, S], U8, "picked_rows")
        v_scales = held([P, PASSES * S], U8, "v_scales")
        w1_scales_raw = held([P, PASSES * H], U8, "w1_scales_raw")
        w1_raw = held([P, PASSES * 2 * H], U8, "w1_raw")
        w1_codes = held([P, PASSES * 2 * H], U8, "w1_codes")
        table = [held([P, T], U32, f"table{a}") for a in range(PASSES)]
        v_codes = [[held([P, HALF], U32, f"v_codes{a}_{u}") for u in range(2)] for a in range(PASSES)]
        w2_raw = [held([P, PACK, H], F32, f"w2_raw{a}") for a in range(PASSES)]
        gain_t = held([P, PACK], F32, "gain_t")
        ones = held([P, 1], F32, "ones")
        shift = held([P, 1], F32, "shift")

        first_row = P - BLOCKS * PASSES
        nc.vector.memset(scale_rows[0:first_row, :].bitcast(I32), 0)
        nc.gpsimd.memset(ones[:], 1.0)
        nc.gpsimd.memset(w1_scales_raw[:].bitcast(I32), 0)
        nc.gpsimd.memset(v_scales[:].bitcast(I32), 0)
        nc.scalar.activation(shift[:], ones[:], ACT.Sin, scale=-ASIN_PI_8)

        def load_table(a):
            words = tab_words[a].rearrange("p t i -> p (t i)").bitcast(I32)
            for c0 in range(0, T, T // 2):
                nc.sync.dma_start(out=table[a][:, c0 : c0 + T // 2].bitcast(I32), in_=words[:, c0 : c0 + T // 2])

        def load_w2(a, width=H):
            rows = w2[a * P * PACK : (a + 1) * P * PACK, :].rearrange("(p j) c -> p j c", j=PACK)
            for c0 in range(0, H, width):
                nc.sync.dma_start(out=w2_raw[a][:, :, c0 : c0 + width], in_=rows[:, :, c0 : c0 + width])

        def plane_rows(planes, quadrant):
            rows = planes[32 * quadrant : 32 * quadrant + 4, :]
            return rows.bitcast(I32).rearrange("r (a c) -> r a c", a=PASSES)

        nc.sync.dma_start(offs_t[:], offs)
        nc.sync.dma_start(
            out=scale_rows[first_row:P, :].bitcast(I32),
            in_=tab_scales.bitcast(I32).rearrange("a q t -> q a t"),
        )
        for quadrant in range(4):
            nc.gpsimd.dma_start(
                out=plane_rows(w1_scales_raw, quadrant),
                in_=w1_scales.bitcast(I32)[:, 4 * quadrant : 4 * quadrant + 4, :].rearrange("a r c -> r a c"),
            )
        load_table(0)

        nc.vector.tensor_copy(picked_rows[:], scale_rows[:].indirect(offs_t[:]))
        for quadrant in range(4):
            row0 = first_row + 4 * PASSES * quadrant
            nc.scalar.dma_start(
                out=plane_rows(v_scales, quadrant), in_=picked_rows[row0 : row0 + 4 * PASSES, :].bitcast(I32)
            )

        load_table(1)
        load_w2(0)
        load_table(2)
        load_w2(1)
        load_w2(2, H // 2)
        nc.sync.dma_start(
            out=w1_raw[:].bitcast(I32).rearrange("p (a c) -> p a c", a=PASSES),
            in_=w1_words.bitcast(I32).rearrange("a p c -> p a c"),
        )
        nc.sync.dma_start(pos1_t[:], pos1)
        nc.sync.dma_start(pos2_t[:], pos2)
        nc.sync.dma_start(pos4_t[:], pos4)
        nc.sync.dma_start(pos3_t[:], pos3)
        with nc.allow_non_contiguous_dma(reason="one gain value a partition"):
            nc.sync.dma_start(out=gain_t[:], in_=gain.rearrange("(c p) -> p c", p=P))

        def gather_words(a):
            for u in range(2):
                cols = slice(u * HALF // LIST_ROWS, (u + 1) * HALF // LIST_ROWS)
                nc.vector.tensor_copy(v_codes[a][u][:], table[a][:].indirect(offs_t[:, cols]))

        w2_bf = [[held([P, P * PACK], BF16, f"w2_bf{a}_{t}") for t in range(PACK)] for a in range(PASSES)]
        w2_codes = [[held([P, P], U32, f"w2_codes{a}_{t}") for t in range(PACK)] for a in range(PASSES)]
        w2_scales = [[held([P, P], U8, f"w2_scales{a}_{t}") for t in range(PACK)] for a in range(PASSES)]

        def round_w2(a, t, copy, blocks=slice(0, BLOCKS)):
            src = w2_raw[a][:].rearrange("p j (g t h l) -> p t g h j l", t=PACK, h=RUN // LINE, l=LINE)[:, t]
            dst = w2_bf[a][t][:].rearrange("p (g h l j) -> p g h j l", h=RUN // LINE, l=LINE, j=PACK)
            copy(out=dst[:, blocks], in_=src[:, blocks])

        def quantise_w2(a, t):
            nc.vector.quantize_mx(out=w2_codes[a][t][:].bitcast(FP8X4), scales=w2_scales[a][t][:], in_=w2_bf[a][t][:])

        def prepare_w2(a, tiles, copy):
            for t in tiles:
                round_w2(a, t, copy)
            for t in tiles:
                quantise_w2(a, t)

        banks = {}

        def piece_width(kind, t):
            return QUARTER if (kind, t) == ("b", 0) else HALF

        def products(kind, t):
            width = piece_width(kind, t)
            for n, j0 in enumerate(range(0, S, width)):
                bank = psum.tile([P, width], F32, name=f"{kind}{t}_{n}", tag=f"{kind}{n % 2}")
                banks[kind, t, j0] = bank
                u, c1 = divmod(j0, HALF)
                for a in range(PASSES):
                    if kind == "f":
                        c0 = a * H + t * P
                        lhsT = w1_codes[:, 2 * c0 : 2 * (c0 + P)].bitcast(FP4X4)
                        lhsT_scale = w1_scales_t[:, c0 : c0 + P]
                    else:
                        lhsT = w2_codes[a][t][:].bitcast(FP8X4)
                        lhsT_scale = w2_scales[a][t][:]
                    nc.tensor.matmul_mx(
                        out=bank[:],
                        lhsT=lhsT,
                        lhsT_scale=lhsT_scale,
                        rhs=v_codes[a][u][:, c1 : c1 + width].bitcast(FP8X4),
                        rhs_scale=v_scales[:, a * S + j0 : a * S + j0 + width],
                        start=(a == 0),
                        stop=(a == PASSES - 1),
                    )

        h = [held([P, S], F32, f"h{t}") for t in range(PACK)]
        a1 = [held([P, P1], F32, f"a1_{t}") for t in range(PACK)]
        work = held([P, PACK * S], F32, "work")
        cos2_first = held([P, S], F32, "cos2_first")

        def gate(t):
            sine = ring.tile([P, S], F32, name="sine")
            square = ring.tile([P, S], F32, name="square", align_bytes=64)
            cos2 = cos2_first[:] if t == 0 else work[:, (t - 1) * S : t * S]
            width = piece_width("b", t)
            span = width if t == 0 else S
            for j0 in range(0, S, width):
                cols = slice(j0, j0 + width)
                nc.scalar.activation(sine[:, cols], banks["b", t, j0][:], ACT.Sin, bias=shift[:], scale=0.25)
                if (j0 + width) % span == 0:
                    done = slice(j0 + width - span, j0 + width)
                    nc.scalar.activation(square[:, done], sine[:, done], ACT.Square)
                    nc.scalar.activation(cos2[:, done], square[:, done], ACT.Square, bias=ones[:], scale=-2.0)
            for j0 in range(0, S, width):
                f_bank = banks["f", t, j0 - j0 % HALF]
                nc.vector.scalar_tensor_tensor(
                    h[t][:, j0 : j0 + width],
                    cos2[:, j0 : j0 + width],
                    2.0,
                    f_bank[:, j0 % HALF : j0 % HALF + width],
                    ALU.mult,
                    ALU.mult,
                )

        def pairs(t):
            first = ring.tile([P, P1], F32, name="first")
            second = ring.tile([P, P1], F32, name="second")
            memo = ring.tile([P, P2], F32, name="memo")
            nc.vector.tensor_copy(first[:], h[t][:].indirect(pos1_t[:]))
            nc.vector.tensor_copy(second[:], h[t][:].indirect(pos2_t[:]))
            nc.vector.tensor_copy(memo[:], h[t][:].indirect(pos4_t[:]))
            nc.vector.tensor_tensor(a1[t][:], first[:], second[:], ALU.max)
            return memo

        def differences(t, memo, pieces):
            width = P2 // pieces
            for j0 in range(0, P2, width):
                picked = a1[t][:].indirect(pos3_t[:, j0 // LIST_ROWS : (j0 + width) // LIST_ROWS])
                a2_cols = work[:, t * S + j0 : t * S + j0 + width]
                nc.vector.tensor_tensor(a2_cols, picked, memo[:, j0 : j0 + width], ALU.subtract)

        gather_words(0)
        w3_raw = held([P, PACK, N], F32, "table0")
        for t in range(PACK):
            nc.sync.dma_start(out=w3_raw[:, t, :], in_=w3.rearrange("(g t i) n -> t g i n", t=PACK, i=RUN)[t])
        gather_words(1)
        prepare_w2(0, range(PACK), nc.vector.tensor_copy)
        w1_scales_t = held([P, PASSES * H], U8, "w2_raw0")
        nc.vector.tensor_copy(
            out=w1_scales_t[:].bitcast(I32).rearrange("p (a t g w) -> p a t g w", a=PASSES, t=PACK, g=BLOCKS),
            in_=w1_scales_raw[:].bitcast(I32).rearrange("p (a g t w) -> p a t g w", a=PASSES, t=PACK, g=BLOCKS),
        )
        gather_words(2)
        prepare_w2(1, (0, 1), nc.vector.tensor_copy)
        prepare_w2(1, (2, 3), nc.scalar.copy)
        for g0 in range(0, BLOCKS, BLOCKS // 2):
            round_w2(2, 0, nc.vector.tensor_copy, slice(g0, g0 + BLOCKS // 2))
        quantise_w2(2, 0)
        prepare_w2(2, (1,), nc.scalar.copy)
        nc.vector.tensor_copy(
            out=w1_codes[:].bitcast(I32).rearrange("p (a t g w) -> p a t g w", a=PASSES, t=PACK, g=BLOCKS),
            in_=w1_raw[:].bitcast(I32).rearrange("p (a g t w) -> p a t g w", a=PASSES, t=PACK, g=BLOCKS),
        )
        prepare_w2(2, (2, 3), nc.vector.tensor_copy)
        for t in (0, 1):
            products("b", t)
            products("f", t)

        w3_codes = held([P, N], U32, "w3_codes")
        w3_scales = held([P, N], U8, "w3_scales")

        memos = {}
        for t in range(PACK):
            gate(t)
            if t + 2 < PACK:
                products("b", t + 2)
                products("f", t + 2)
            if t > 0:
                differences(t - 1, memos[t - 1], 1)
            if t == PACK - 1:
                w3_bf = ring.tile([P, N * PACK], BF16, name="square", align_bytes=64)
                nc.scalar.copy(
                    out=w3_bf[:].rearrange("p (c l j) -> p c j l", l=LINE, j=PACK),
                    in_=w3_raw[:].rearrange("p j (c l) -> p c j l", l=LINE),
                )
            memos[t] = pairs(t)
        nc.vector.quantize_mx(out=w3_codes[:].bitcast(FP8X4), scales=w3_scales[:], in_=w3_bf[:])

        differences(PACK - 1, memos[PACK - 1], 2)
        a2_bf = [held([P, P * PACK], BF16, f"a2_bf{u}") for u in range(2)]
        a2_codes = [held([P, P], U32, f"a2_codes{u}") for u in range(2)]
        a2_scales = [held([P, P], U8, f"a2_scales{u}") for u in range(2)]
        a2 = work[:].rearrange("p (t c l) -> p c t l", t=PACK, l=LINE)
        for u in range(2):
            nc.vector.tensor_copy(
                out=a2_bf[u][:].rearrange("p (c l t) -> p c t l", l=LINE, t=PACK),
                in_=a2[:, u * P // LINE : (u + 1) * P // LINE],
            )
        for u in range(2):
            nc.vector.quantize_mx(out=a2_codes[u][:].bitcast(FP8X4), scales=a2_scales[u][:], in_=a2_bf[u][:])

        out_view = out.rearrange("(c p) j -> p c j", p=P)
        groups = [(u, range(c0, c0 + 2)) for u in range(2) for c0 in (0, 2)]
        for n, ((u, chunks), tag) in enumerate(zip(groups, ("b0", "b1", "f0", "f1"))):
            y = psum.tile([P, len(chunks), P], F32, name=f"y{n}", tag=tag)
            bent = held([P, len(chunks), P], F32, f"bent{n}")
            lead = held([P, len(chunks), P], F32, f"lead{n}")
            for m, c in enumerate(chunks):
                nc.tensor.matmul_mx(
                    out=y[:, m, :],
                    lhsT=w3_codes[:, c * P : (c + 1) * P].bitcast(FP8X4),
                    lhsT_scale=w3_scales[:, c * P : (c + 1) * P],
                    rhs=a2_codes[u][:].bitcast(FP8X4),
                    rhs_scale=a2_scales[u][:],
                    start=True,
                    stop=True,
                )
            nc.scalar.activation(bent[:], y[:], ACT.Tanh)
            for m, c in enumerate(chunks):
                nc.vector.tensor_scalar(lead[:, m, :], bent[:, m, :], gain_t[:, c : c + 1], None, ALU.mult)
            nc.sync.dma_start(out=out_view[:, chunks.start : chunks.stop, u * P : (u + 1) * P], in_=lead[:])
